import numpy as np
import ml_dtypes


def mxq(x, axis, fmt="e4m3"):
    dtype, down = {"e4m3": (ml_dtypes.float8_e4m3fn, 7), "e5m2": (ml_dtypes.float8_e5m2, 14)}[fmt]
    v = np.moveaxis(np.asarray(x, np.float32).astype(ml_dtypes.bfloat16).astype(np.float64), axis, -1)
    blocks = v.reshape(v.shape[:-1] + (-1, 32))
    amax = np.abs(blocks).max(-1, keepdims=True)
    byte = np.maximum(np.where(amax > 0, np.frexp(amax)[1] - 1 + 127, 0) - down, 1)
    scale = np.exp2(byte - 127.0)
    codes = (blocks / scale).astype(np.float32).astype(dtype).astype(np.float64)
    return np.moveaxis((codes * scale).reshape(v.shape), -1, axis)


WIDE = False


def mx_kscale(k):
    if not WIDE:
        return np.ones(k)
    levels = np.array([30, -30])
    if k % 512:
        return np.exp2(np.random.permutation(np.resize(levels, k // 32))).repeat(32)
    a = np.empty((k // 512, 16))
    for p in range(k // 512):
        a[p, :8] = np.random.permutation(np.resize(levels, 8))
        for g in range(8):
            far = levels[np.abs(levels - a[p, g]) >= 10]
            a[p, g + 8] = far[np.random.randint(len(far))]
    return np.exp2(a.ravel()).repeat(32)


def f64(x):
    return np.asarray(x).astype(np.float64)


def striped(idx):
    return np.tile(np.asarray(idx).reshape(-1, 16).T, (8, 1)).astype(np.uint16)


def unstriped(offs):
    return offs[:16].T.reshape(-1).astype(np.int64)


E2M1 = np.array([0.0, 0.5, 1.0, 1.5, 2.0, 3.0, 4.0, 6.0, -0.0, -0.5, -1.0, -1.5, -2.0, -3.0, -4.0, -6.0])


def pack_weight(w, fmt):
    k, n = w.shape
    w = f64(np.asarray(w, np.float32).astype(ml_dtypes.bfloat16)).reshape(k // 32, 32, n)
    amax = np.abs(w).max(1)
    if fmt in ("e4m3", "e5m2"):
        byte = np.frexp(amax)[1] - 1 + 127 - (7 if fmt == "e4m3" else 14)
    else:
        mant, ex = np.frexp(amax / 6.0)
        byte = np.where(mant > 0.5, ex, ex - 1) + 127
    byte = np.clip(np.where(amax > 0, byte, 1), 1, 254)
    scaled = (w * np.exp2(127.0 - byte)[:, None, :]).reshape(k, n).astype(np.float32)
    by_word = np.ascontiguousarray(scaled.reshape(k // 512, 128, 4, n).transpose(0, 1, 3, 2))
    if fmt in ("e4m3", "e5m2"):
        words = by_word.astype(ml_dtypes.float8_e4m3fn if fmt == "e4m3" else ml_dtypes.float8_e5m2).view(np.uint8)
    else:
        c = by_word.astype(ml_dtypes.float4_e2m1fn).view(np.uint8) & 0xF
        words = (c[..., 0::2] | (c[..., 1::2] << 4)).reshape(k // 512, 128, 2 * n)
    return np.ascontiguousarray(words), np.ascontiguousarray(byte.astype(np.uint8).reshape(k // 512, 16, n))


def unpack_weight(words, scales, fmt):
    g, _, n = scales.shape
    words = np.ascontiguousarray(words).reshape(g, 128, n, -1)
    if fmt in ("e4m3", "e5m2"):
        vals = words.view(ml_dtypes.float8_e4m3fn if fmt == "e4m3" else ml_dtypes.float8_e5m2).astype(np.float64)
    else:
        nib = np.empty((g, 128, n, 4), np.uint8)
        nib[..., 0::2] = words & 0xF
        nib[..., 1::2] = words >> 4
        vals = E2M1[nib]
    vals = vals * np.repeat(np.exp2(scales.astype(np.float64) - 127.0), 8, axis=1)[..., None]
    return vals.transpose(0, 1, 3, 2).reshape(g * 512, n)


K, T, J, I, R, G, S = 512, 512, 256, 256, 512, 32, 32


def setup_inputs():
    n = np.random.standard_normal
    idx = np.random.permutation(T)[:J]
    idx2 = np.random.permutation(T)[:I]
    fk = mx_kscale(K)
    fr = mx_kscale(R)
    xtp = pack_weight(n((K, T)) / fk[:, None], "e5m2")
    wap = pack_weight(n((K, R)) * 0.5 / np.sqrt(K) * fk[:, None] * fr, "e4m3")
    wbp = pack_weight(n((K, R)) * 1 / np.sqrt(K) * fk[:, None] / fr, "e2m1")
    return {
        "xt_words": xtp[0],
        "xt_scales": xtp[1],
        "wa_words": wap[0],
        "wa_scales": wap[1],
        "wb_words": wbp[0],
        "wb_scales": wbp[1],
        "bi": (np.random.uniform(-15.0, 15.0, (1, I))).astype(np.float32),
        "offs": striped(idx),
        "offs2": striped(idx2),
    }


def reference(xt_words, xt_scales, wa_words, wa_scales, wb_words, wb_scales, bi, offs, offs2):
    idx = unstriped(offs)
    idx2 = unstriped(offs2)
    xtu = unpack_weight(xt_words, xt_scales, "e5m2")
    wau = unpack_weight(wa_words, wa_scales, "e4m3")
    wbu = unpack_weight(wb_words, wb_scales, "e2m1")
    xtidxg = xtu[:, idx]
    za = wau.T @ xtidxg
    ya1 = np.pad(za, ((0, 0), (1, 0)))[:, :J]
    ha = za - 0.6 * ya1
    xtidx2g = xtu[:, idx2]
    zb = wbu.T @ xtidx2g
    mb1 = zb.reshape(R, G, I // G).mean(axis=2)
    mb2 = np.repeat(mb1, I // G, axis=1)
    hb = zb - mb2
    haq = mxq(ha, 0, "e5m2")
    hbq = mxq(hb, 0, "e4m3")
    a0 = haq.T @ hbq
    a = a0 + f64(bi)
    g1 = a.reshape(J, S, I // S).max(axis=2)
    y = 0.04 * g1
    return y

@@ -1,0 +1,179 @@
+from contextlib import ExitStack
+
+import concourse.mybir as mybir
+
+F32 = mybir.dt.float32
+BF16 = mybir.dt.bfloat16
+I32 = mybir.dt.int32
+U32 = mybir.dt.uint32
+U16 = mybir.dt.uint16
+U8 = mybir.dt.uint8
+E4M3 = mybir.dt.float8_e4m3fn_x4
+E5M2 = mybir.dt.float8_e5m2_x4
+E2M1 = mybir.dt.float4_e2m1fn_x4
+ALU = mybir.AluOpType
+COPY = mybir.ActivationFunctionType.Copy
+AXIS_X = mybir.AxisListType.X
+
+P = 128
+T = 512
+R = 512
+J = 256
+HALF = 128
+PACK = 4
+BUNDLE = 8
+FLOPS = 335544320
+
+
+def tile_list_meet_lagged_levelled_bundlemax_kernel(tc, xt_words, xt_scales, wa_words, wa_scales, wb_words, wb_scales, bi, offs, offs2, out):
+    nc = tc.nc
+    with ExitStack() as ctx:
+        sb = ctx.enter_context(tc.tile_pool(name="sb", bufs=1))
+        ps = ctx.enter_context(tc.psum_pool(name="ps", bufs=1))
+
+        def tile(shape, dtype, name):
+            return sb.tile(shape, dtype, name=name, align_bytes=64)
+
+        def load_plane(queue, plane, scales):
+            rows = scales[0].bitcast(I32)
+            for q in range(4):
+                queue.dma_start(plane[32 * q : 32 * q + 4, :].bitcast(I32), rows[4 * q : 4 * q + 4, :])
+
+        list_a = sb.tile([P, J // 16], U16, name="list_a")
+        list_b = sb.tile([P, J // 16], U16, name="list_b")
+        x_words = tile([P, T], U32, "x_words")
+        x_plane = tile([P, T], U8, "x_plane")
+        wa_raw = tile([P, R], U32, "wa_raw")
+        wb_raw = tile([P, R // 2], U32, "wb_raw")
+        wa_plane_raw = tile([P, R], U8, "wa_plane_raw")
+        wb_plane_raw = tile([P, R], U8, "wb_plane_raw")
+        bias_raw = tile([P, J], F32, "bias_raw")
+        lag = tile([P, J, PACK], F32, "lag")
+
+        nc.vector.memset(x_plane[:].bitcast(I32), 0)
+        nc.vector.memset(wb_plane_raw[:].bitcast(I32), 0)
+        nc.vector.memset(wa_plane_raw[:].bitcast(I32), 0)
+        nc.vector.memset(lag[:, 0, :], 0.0)
+
+        nc.sync.dma_start(list_b[:], offs2)
+        nc.sync.dma_start(x_words[:].bitcast(I32), xt_words[0].rearrange("p n t -> p (n t)").bitcast(I32))
+        load_plane(nc.scalar, x_plane, xt_scales)
+        nc.sync.dma_start(list_a[:], offs)
+        nc.sync.dma_start(wb_raw[:].bitcast(I32), wb_words[0].bitcast(I32))
+        load_plane(nc.sync, wb_plane_raw, wb_scales)
+        nc.sync.dma_start(wa_raw[:].bitcast(I32), wa_words[0].rearrange("p n t -> p (n t)").bitcast(I32))
+        load_plane(nc.sync, wa_plane_raw, wa_scales)
+        nc.sync.dma_start(bias_raw[:], bi[0].partition_broadcast(P))
+
+        xb_words = tile([P, J], U32, "xb_words")
+        xb_plane = tile([P, J], U8, "xb_plane")
+        xa_words = tile([P, J], U32, "xa_words")
+        xa_plane = tile([P, J], U8, "xa_plane")
+        nc.vector.tensor_copy(xb_words[:], x_words[:].indirect(list_b[:]))
+        nc.vector.tensor_copy(xb_plane[:], x_plane[:].indirect(list_b[:]))
+        nc.vector.tensor_copy(xa_words[:], x_words[:].indirect(list_a[:]))
+        nc.vector.tensor_copy(xa_plane[:], x_plane[:].indirect(list_a[:]))
+
+        def deal(dst, src):
+            nc.scalar.copy(dst.rearrange("p (t g u) -> p t g u", t=PACK, g=16), src.rearrange("p (g t u) -> p t g u", t=PACK, g=16))
+
+        wb_dealt = tile([P, 2 * R], U8, "wb_dealt")
+        wb_plane = tile([P, R], U8, "wb_plane")
+        wa_dealt = tile([P, R], U32, "wa_dealt")
+        wa_plane = tile([P, R], U8, "wa_plane")
+        deal(wb_dealt[:].bitcast(U32), wb_raw[:])
+        deal(wb_plane[:].bitcast(U32), wb_plane_raw[:].bitcast(U32))
+        deal(wa_dealt[:], wa_raw[:])
+        deal(wa_plane[:].bitcast(U32), wa_plane_raw[:].bitcast(U32))
+
+        zb = [ps.tile([P, PACK, HALF], F32, name="zb%d" % h) for h in range(2)]
+        za = [ps.tile([P, PACK, HALF], F32, name="za%d" % h) for h in range(2)]
+        for h in range(2):
+            cols = slice(HALF * h, HALF * (h + 1))
+            for t in range(PACK):
+                nc.tensor.matmul_mx(
+                    out=zb[h][:, t, :],
+                    lhsT=wb_dealt[:, 2 * P * t : 2 * P * (t + 1)].bitcast(E2M1),
+                    lhsT_scale=wb_plane[:, P * t : P * (t + 1)],
+                    rhs=xb_words[:, cols].bitcast(E5M2),
+                    rhs_scale=xb_plane[:, cols],
+                    start=True,
+                    stop=True,
+                )
+        for h in range(2):
+            cols = slice(HALF * h, HALF * (h + 1))
+            for t in range(PACK):
+                nc.tensor.matmul_mx(
+                    out=za[h][:, t, :],
+                    lhsT=wa_dealt[:, P * t : P * (t + 1)].bitcast(E4M3),
+                    lhsT_scale=wa_plane[:, P * t : P * (t + 1)],
+                    rhs=xa_words[:, cols].bitcast(E5M2),
+                    rhs_scale=xa_plane[:, cols],
+                    start=True,
+                    stop=True,
+                )
+
+        groups = HALF // BUNDLE
+        sums = [tile([P, groups, PACK], F32, "sums%d" % h) for h in range(2)]
+        means = [tile([P, groups, PACK], F32, "means%d" % h) for h in range(2)]
+        hb = tile([P, J, PACK], BF16, "hb")
+        for h in range(2):
+            nc.vector.tensor_reduce(
+                out=sums[h][:], in_=zb[h][:].rearrange("p t (g u) -> p g t u", u=BUNDLE), axis=AXIS_X, op=ALU.add
+            )
+            nc.gpsimd.tensor_scalar(means[h][:], sums[h][:], 1.0 / BUNDLE, 0.0, ALU.mult, ALU.add)
+        for h in range(2):
+            nc.vector.tensor_tensor(
+                hb[:, HALF * h : HALF * (h + 1), :].rearrange("p (g u) t -> p g u t", u=BUNDLE),
+                zb[h][:].rearrange("p t (g u) -> p g u t", u=BUNDLE),
+                means[h][:].unsqueeze(2).to_broadcast([P, groups, BUNDLE, PACK]),
+                ALU.subtract,
+            )
+
+        nc.scalar.activation(lag[:, 1 : HALF + 1, :], za[0][:].rearrange("p t j -> p j t"), COPY, scale=-0.6)
+        nc.scalar.activation(lag[:, HALF + 1 : J, :], za[1][:, :, 0 : HALF - 1].rearrange("p t j -> p j t"), COPY, scale=-0.6)
+        bias = tile([P, J], F32, "bias")
+        nc.scalar.activation(bias[:], bias_raw[:], COPY, scale=0.04)
+
+        ha = [tile([P, HALF, PACK], BF16, "ha%d" % h) for h in range(2)]
+        ha_codes = [tile([P, HALF], U32, "ha_codes%d" % h) for h in range(2)]
+        ha_plane = [tile([P, HALF], U8, "ha_plane%d" % h) for h in range(2)]
+        hb_codes = tile([P, J], U32, "hb_codes")
+        hb_plane = tile([P, J], U8, "hb_plane")
+        score = [ps.tile([P, J], F32, name="score%d" % h) for h in range(2)]
+        biased = [tile([P, J], F32, "biased%d" % h) for h in range(2)]
+        best = [tile([P, J // BUNDLE], F32, "best%d" % h) for h in range(2)]
+
+        def make_ha(h):
+            nc.vector.tensor_tensor(ha[h][:], za[h][:].rearrange("p t j -> p j t"), lag[:, HALF * h : HALF * (h + 1), :], ALU.add)
+
+        def meet(h):
+            nc.vector.quantize_mx(out=ha_codes[h][:].bitcast(E5M2), scales=ha_plane[h][:], in_=ha[h][:].rearrange("p j t -> p (j t)"))
+            nc.tensor.matmul_mx(
+                out=score[h][:],
+                lhsT=ha_codes[h][:].bitcast(E5M2),
+                lhsT_scale=ha_plane[h][:],
+                rhs=hb_codes[:].bitcast(E4M3),
+                rhs_scale=hb_plane[:],
+                start=True,
+                stop=True,
+            )
+
+        def add_bias(h):
+            nc.vector.scalar_tensor_tensor(biased[h][:], score[h][:], 0.04, bias[:], ALU.mult, ALU.add)
+
+        def keep_best(h):
+            nc.vector.tensor_reduce(
+                out=best[h][:], in_=biased[h][:].rearrange("p (s u) -> p s u", u=BUNDLE), axis=AXIS_X, op=ALU.max
+            )
+            nc.sync.dma_start(out[HALF * h : HALF * (h + 1), :], best[h][:])
+
+        make_ha(0)
+        nc.vector.quantize_mx(out=hb_codes[:].bitcast(E4M3), scales=hb_plane[:], in_=hb[:].rearrange("p i t -> p (i t)"))
+        meet(0)
+        make_ha(1)
+        add_bias(0)
+        meet(1)
+        keep_best(0)
+        add_bias(1)
+        keep_best(1)

@@ -12,7 +12,6 @@ E4M3 = mybir.dt.float8_e4m3fn_x4
 E5M2 = mybir.dt.float8_e5m2_x4
 E2M1 = mybir.dt.float4_e2m1fn_x4
 ALU = mybir.AluOpType
-COPY = mybir.ActivationFunctionType.Copy
 AXIS_X = mybir.AxisListType.X
 
 P = 128
@@ -31,13 +30,14 @@ def tile_list_meet_lagged_levelled_bundlemax_kernel(tc, xt_words, xt_scales, wa_
         sb = ctx.enter_context(tc.tile_pool(name="sb", bufs=1))
         ps = ctx.enter_context(tc.psum_pool(name="ps", bufs=1))
 
-        def tile(shape, dtype, name):
-            return sb.tile(shape, dtype, name=name, align_bytes=64)
+        def tile(shape, dtype, name, tag=None):
+            return sb.tile(shape, dtype, name=name, tag=tag or name, align_bytes=64)
 
-        def load_plane(queue, plane, scales):
+        def load_plane(queues, plane, scales):
             rows = scales[0].bitcast(I32)
-            for q in range(4):
-                queue.dma_start(plane[32 * q : 32 * q + 4, :].bitcast(I32), rows[4 * q : 4 * q + 4, :])
+            for q, queue in enumerate(queues):
+                four = rows[4 * q : 4 * q + 4, :].unsqueeze(0).to_broadcast([8, 4, T // 4])
+                queue.dma_start(plane[32 * q : 32 * (q + 1), :].bitcast(I32), four)
 
         list_a = sb.tile([P, J // 16], U16, name="list_a")
         list_b = sb.tile([P, J // 16], U16, name="list_b")
@@ -48,41 +48,39 @@ def tile_list_meet_lagged_levelled_bundlemax_kernel(tc, xt_words, xt_scales, wa_
         wa_plane_raw = tile([P, R], U8, "wa_plane_raw")
         wb_plane_raw = tile([P, R], U8, "wb_plane_raw")
         bias_raw = tile([P, J], F32, "bias_raw")
-        lag = tile([P, J, PACK], F32, "lag")
+        lag = [tile([P, HALF, PACK], F32, "lag%d" % h) for h in range(2)]
 
-        nc.vector.memset(x_plane[:].bitcast(I32), 0)
-        nc.vector.memset(wb_plane_raw[:].bitcast(I32), 0)
-        nc.vector.memset(wa_plane_raw[:].bitcast(I32), 0)
-        nc.vector.memset(lag[:, 0, :], 0.0)
+        nc.vector.memset(lag[0][:, 0, :], 0.0)
 
         nc.sync.dma_start(list_b[:], offs2)
-        nc.sync.dma_start(x_words[:].bitcast(I32), xt_words[0].rearrange("p n t -> p (n t)").bitcast(I32))
-        load_plane(nc.scalar, x_plane, xt_scales)
+        load_plane([nc.sync, nc.sync, nc.scalar, nc.scalar], x_plane, xt_scales)
         nc.sync.dma_start(list_a[:], offs)
+        nc.scalar.dma_start(x_words[:].bitcast(I32), xt_words[0].rearrange("p n t -> p (n t)").bitcast(I32))
         nc.sync.dma_start(wb_raw[:].bitcast(I32), wb_words[0].bitcast(I32))
-        load_plane(nc.sync, wb_plane_raw, wb_scales)
+        load_plane([nc.sync] * 3 + [nc.gpsimd], wb_plane_raw, wb_scales)
         nc.sync.dma_start(wa_raw[:].bitcast(I32), wa_words[0].rearrange("p n t -> p (n t)").bitcast(I32))
-        load_plane(nc.sync, wa_plane_raw, wa_scales)
+        load_plane([nc.sync] * 4, wa_plane_raw, wa_scales)
         nc.sync.dma_start(bias_raw[:], bi[0].partition_broadcast(P))
 
         xb_words = tile([P, J], U32, "xb_words")
         xb_plane = tile([P, J], U8, "xb_plane")
         xa_words = tile([P, J], U32, "xa_words")
         xa_plane = tile([P, J], U8, "xa_plane")
-        nc.vector.tensor_copy(xb_words[:], x_words[:].indirect(list_b[:]))
         nc.vector.tensor_copy(xb_plane[:], x_plane[:].indirect(list_b[:]))
-        nc.vector.tensor_copy(xa_words[:], x_words[:].indirect(list_a[:]))
         nc.vector.tensor_copy(xa_plane[:], x_plane[:].indirect(list_a[:]))
+        for h in range(2):
+            nc.vector.tensor_copy(xb_words[:, HALF * h : HALF * (h + 1)], x_words[:].indirect(list_b[:, 8 * h : 8 * (h + 1)]))
+        nc.vector.tensor_copy(xa_words[:], x_words[:].indirect(list_a[:]))
 
         def deal(dst, src):
             nc.scalar.copy(dst.rearrange("p (t g u) -> p t g u", t=PACK, g=16), src.rearrange("p (g t u) -> p t g u", t=PACK, g=16))
 
         wb_dealt = tile([P, 2 * R], U8, "wb_dealt")
         wb_plane = tile([P, R], U8, "wb_plane")
-        wa_dealt = tile([P, R], U32, "wa_dealt")
         wa_plane = tile([P, R], U8, "wa_plane")
         deal(wb_dealt[:].bitcast(U32), wb_raw[:])
         deal(wb_plane[:].bitcast(U32), wb_plane_raw[:].bitcast(U32))
+        wa_dealt = tile([P, R], U32, "wa_dealt")
         deal(wa_dealt[:], wa_raw[:])
         deal(wa_plane[:].bitcast(U32), wa_plane_raw[:].bitcast(U32))
 
@@ -130,50 +128,55 @@ def tile_list_meet_lagged_levelled_bundlemax_kernel(tc, xt_words, xt_scales, wa_
                 ALU.subtract,
             )
 
-        nc.scalar.activation(lag[:, 1 : HALF + 1, :], za[0][:].rearrange("p t j -> p j t"), COPY, scale=-0.6)
-        nc.scalar.activation(lag[:, HALF + 1 : J, :], za[1][:, :, 0 : HALF - 1].rearrange("p t j -> p j t"), COPY, scale=-0.6)
+        nc.scalar.copy(lag[0][:, 1:HALF, :], za[0][:, :, 0 : HALF - 1].rearrange("p t j -> p j t"))
+        nc.scalar.copy(lag[1][:, 0, :], za[0][:, :, HALF - 1])
+        nc.scalar.copy(lag[1][:, 1:HALF, :], za[1][:, :, 0 : HALF - 1].rearrange("p t j -> p j t"))
         bias = tile([P, J], F32, "bias")
-        nc.scalar.activation(bias[:], bias_raw[:], COPY, scale=0.04)
+        nc.gpsimd.tensor_scalar(bias[:], bias_raw[:], 0.04, 0.0, ALU.mult, ALU.add)
 
-        ha = [tile([P, HALF, PACK], BF16, "ha%d" % h) for h in range(2)]
         ha_codes = [tile([P, HALF], U32, "ha_codes%d" % h) for h in range(2)]
         ha_plane = [tile([P, HALF], U8, "ha_plane%d" % h) for h in range(2)]
-        hb_codes = tile([P, J], U32, "hb_codes")
         hb_plane = tile([P, J], U8, "hb_plane")
-        score = [ps.tile([P, J], F32, name="score%d" % h) for h in range(2)]
-        biased = [tile([P, J], F32, "biased%d" % h) for h in range(2)]
         best = [tile([P, J // BUNDLE], F32, "best%d" % h) for h in range(2)]
 
-        def make_ha(h):
-            nc.vector.tensor_tensor(ha[h][:], za[h][:].rearrange("p t j -> p j t"), lag[:, HALF * h : HALF * (h + 1), :], ALU.add)
-
-        def meet(h):
-            nc.vector.quantize_mx(out=ha_codes[h][:].bitcast(E5M2), scales=ha_plane[h][:], in_=ha[h][:].rearrange("p j t -> p (j t)"))
-            nc.tensor.matmul_mx(
-                out=score[h][:],
-                lhsT=ha_codes[h][:].bitcast(E5M2),
-                lhsT_scale=ha_plane[h][:],
-                rhs=hb_codes[:].bitcast(E4M3),
-                rhs_scale=hb_plane[:],
-                start=True,
-                stop=True,
+        def make_ha(h, tag):
+            ha = tile([P, HALF, PACK], BF16, "ha%d" % h, tag=tag)
+            nc.vector.scalar_tensor_tensor(
+                ha[:], lag[h][:], -0.6, za[h][:].rearrange("p t j -> p j t"), ALU.mult, ALU.add
             )
+            return ha
 
-        def add_bias(h):
-            nc.vector.scalar_tensor_tensor(biased[h][:], score[h][:], 0.04, bias[:], ALU.mult, ALU.add)
+        def quantize_ha(h, ha):
+            nc.vector.quantize_mx(out=ha_codes[h][:].bitcast(E5M2), scales=ha_plane[h][:], in_=ha[:].rearrange("p j t -> p (j t)"))
 
-        def keep_best(h):
-            nc.vector.tensor_reduce(
-                out=best[h][:], in_=biased[h][:].rearrange("p (s u) -> p s u", u=BUNDLE), axis=AXIS_X, op=ALU.max
-            )
+        def meet(h, pieces):
+            width = J // pieces
+            biased = []
+            for c in range(pieces):
+                cols = slice(width * c, width * (c + 1))
+                score = ps.tile([P, width], F32, name="score%d_%d" % (h, c))
+                nc.tensor.matmul_mx(
+                    out=score[:],
+                    lhsT=ha_codes[h][:].bitcast(E5M2),
+                    lhsT_scale=ha_plane[h][:],
+                    rhs=hb_codes[:, cols].bitcast(E4M3),
+                    rhs_scale=hb_plane[:, cols],
+                    start=True,
+                    stop=True,
+                )
+                biased.append(tile([P, width], F32, "biased%d_%d" % (h, c)))
+                nc.vector.scalar_tensor_tensor(biased[c][:], score[:], 0.04, bias[:, cols], ALU.mult, ALU.add)
+            for c in range(pieces):
+                sets = slice(width // BUNDLE * c, width // BUNDLE * (c + 1))
+                nc.vector.tensor_reduce(
+                    out=best[h][:, sets], in_=biased[c][:].rearrange("p (s u) -> p s u", u=BUNDLE), axis=AXIS_X, op=ALU.max
+                )
             nc.sync.dma_start(out[HALF * h : HALF * (h + 1), :], best[h][:])
 
-        make_ha(0)
+        ha0 = make_ha(0, "ha0")
+        hb_codes = tile([P, J], U32, "hb_codes", tag="lag0")
         nc.vector.quantize_mx(out=hb_codes[:].bitcast(E4M3), scales=hb_plane[:], in_=hb[:].rearrange("p i t -> p (i t)"))
-        meet(0)
-        make_ha(1)
-        add_bias(0)
-        meet(1)
-        keep_best(0)
-        add_bias(1)
-        keep_best(1)
+        quantize_ha(0, ha0)
+        quantize_ha(1, make_ha(1, "hb"))
+        meet(0, 1)
+        meet(1, 2)

@@ -1,6 +1,7 @@
 from contextlib import ExitStack
 
 import concourse.mybir as mybir
+from concourse.masks import make_identity
 
 F32 = mybir.dt.float32
 BF16 = mybir.dt.bfloat16
@@ -12,6 +13,7 @@ E4M3 = mybir.dt.float8_e4m3fn_x4
 E5M2 = mybir.dt.float8_e5m2_x4
 E2M1 = mybir.dt.float4_e2m1fn_x4
 ALU = mybir.AluOpType
+COPY = mybir.ActivationFunctionType.Copy
 AXIS_X = mybir.AxisListType.X
 
 P = 128
@@ -39,6 +41,11 @@ def tile_list_meet_lagged_levelled_bundlemax_kernel(tc, xt_words, xt_scales, wa_
                 four = rows[4 * q : 4 * q + 4, :].unsqueeze(0).to_broadcast([8, 4, T // 4])
                 queue.dma_start(plane[32 * q : 32 * (q + 1), :].bitcast(I32), four)
 
+        def load_rows(queues, plane, scales):
+            rows = scales[0].bitcast(I32)
+            for q, queue in enumerate(queues):
+                queue.dma_start(plane[32 * q : 32 * q + 4, :].bitcast(I32), rows[4 * q : 4 * q + 4, :])
+
         list_a = sb.tile([P, J // 16], U16, name="list_a")
         list_b = sb.tile([P, J // 16], U16, name="list_b")
         x_words = tile([P, T], U32, "x_words")
@@ -47,9 +54,12 @@ def tile_list_meet_lagged_levelled_bundlemax_kernel(tc, xt_words, xt_scales, wa_
         wb_raw = tile([P, R // 2], U32, "wb_raw")
         wa_plane_raw = tile([P, R], U8, "wa_plane_raw")
         wb_plane_raw = tile([P, R], U8, "wb_plane_raw")
-        bias_raw = tile([P, J], F32, "bias_raw")
+        bias_raw = tile([P, 2], F32, "bias_raw")
+        identity = tile([P, P], F32, "identity")
         lag = [tile([P, HALF, PACK], F32, "lag%d" % h) for h in range(2)]
 
+        nc.vector.memset(wb_plane_raw[:].bitcast(I32), 0)
+        nc.vector.memset(wa_plane_raw[:].bitcast(I32), 0)
         nc.vector.memset(lag[0][:, 0, :], 0.0)
 
         nc.sync.dma_start(list_b[:], offs2)
@@ -57,10 +67,11 @@ def tile_list_meet_lagged_levelled_bundlemax_kernel(tc, xt_words, xt_scales, wa_
         nc.sync.dma_start(list_a[:], offs)
         nc.scalar.dma_start(x_words[:].bitcast(I32), xt_words[0].rearrange("p n t -> p (n t)").bitcast(I32))
         nc.sync.dma_start(wb_raw[:].bitcast(I32), wb_words[0].bitcast(I32))
-        load_plane([nc.sync] * 3 + [nc.gpsimd], wb_plane_raw, wb_scales)
+        load_rows([nc.sync] * 4, wb_plane_raw, wb_scales)
         nc.sync.dma_start(wa_raw[:].bitcast(I32), wa_words[0].rearrange("p n t -> p (n t)").bitcast(I32))
-        load_plane([nc.sync] * 4, wa_plane_raw, wa_scales)
-        nc.sync.dma_start(bias_raw[:], bi[0].partition_broadcast(P))
+        load_rows([nc.sync] * 3 + [nc.gpsimd], wa_plane_raw, wa_scales)
+        nc.sync.dma_start(bias_raw[:], bi[0].rearrange("(p c) -> p c", c=2))
+        make_identity(nc, identity[:])
 
         xb_words = tile([P, J], U32, "xb_words")
         xb_plane = tile([P, J], U8, "xb_plane")
@@ -131,8 +142,13 @@ def tile_list_meet_lagged_levelled_bundlemax_kernel(tc, xt_words, xt_scales, wa_
         nc.scalar.copy(lag[0][:, 1:HALF, :], za[0][:, :, 0 : HALF - 1].rearrange("p t j -> p j t"))
         nc.scalar.copy(lag[1][:, 0, :], za[0][:, :, HALF - 1])
         nc.scalar.copy(lag[1][:, 1:HALF, :], za[1][:, :, 0 : HALF - 1].rearrange("p t j -> p j t"))
+        bias_scaled = tile([P, 2], F32, "bias_scaled", tag="wa_plane")
+        nc.scalar.activation(bias_scaled[:], bias_raw[:], COPY, scale=0.04)
+        spread = ps.tile([P, 2, P], F32, name="spread", tag="score1_1")
+        for c in range(2):
+            nc.tensor.transpose(spread[:, c, :], bias_scaled[:, c : c + 1].to_broadcast([P, P]), identity[:])
         bias = tile([P, J], F32, "bias")
-        nc.gpsimd.tensor_scalar(bias[:], bias_raw[:], 0.04, 0.0, ALU.mult, ALU.add)
+        nc.scalar.copy(bias[:].rearrange("p (n c) -> p n c", c=2), spread[:].rearrange("p c n -> p n c"))
 
         ha_codes = [tile([P, HALF], U32, "ha_codes%d" % h) for h in range(2)]
         ha_plane = [tile([P, HALF], U8, "ha_plane%d" % h) for h in range(2)]
@@ -164,7 +180,7 @@ def tile_list_meet_lagged_levelled_bundlemax_kernel(tc, xt_words, xt_scales, wa_
                     start=True,
                     stop=True,
                 )
-                biased.append(tile([P, width], F32, "biased%d_%d" % (h, c)))
+                biased.append(tile([P, width], F32, "biased%d_%d" % (h, c), tag="hb" if (h, c) == (0, 1) else None))
                 nc.vector.scalar_tensor_tensor(biased[c][:], score[:], 0.04, bias[:, cols], ALU.mult, ALU.add)
             for c in range(pieces):
                 sets = slice(width // BUNDLE * c, width // BUNDLE * (c + 1))
@@ -178,5 +194,5 @@ def tile_list_meet_lagged_levelled_bundlemax_kernel(tc, xt_words, xt_scales, wa_
         nc.vector.quantize_mx(out=hb_codes[:].bitcast(E4M3), scales=hb_plane[:], in_=hb[:].rearrange("p i t -> p (i t)"))
         quantize_ha(0, ha0)
         quantize_ha(1, make_ha(1, "hb"))
-        meet(0, 1)
+        meet(0, 2)
         meet(1, 2)

from contextlib import ExitStack

import concourse.mybir as mybir
from concourse.masks import make_identity

F32 = mybir.dt.float32
BF16 = mybir.dt.bfloat16
I32 = mybir.dt.int32
U32 = mybir.dt.uint32
U16 = mybir.dt.uint16
U8 = mybir.dt.uint8
E4M3 = mybir.dt.float8_e4m3fn_x4
E5M2 = mybir.dt.float8_e5m2_x4
E2M1 = mybir.dt.float4_e2m1fn_x4
ALU = mybir.AluOpType
COPY = mybir.ActivationFunctionType.Copy
AXIS_X = mybir.AxisListType.X

P = 128
T = 512
R = 512
J = 256
HALF = 128
PACK = 4
BUNDLE = 8
FLOPS = 335544320


def tile_list_meet_lagged_levelled_bundlemax_kernel(tc, xt_words, xt_scales, wa_words, wa_scales, wb_words, wb_scales, bi, offs, offs2, out):
    nc = tc.nc
    with ExitStack() as ctx:
        sb = ctx.enter_context(tc.tile_pool(name="sb", bufs=1))
        ps = ctx.enter_context(tc.psum_pool(name="ps", bufs=1))

        def tile(shape, dtype, name, tag=None):
            return sb.tile(shape, dtype, name=name, tag=tag or name, align_bytes=64)

        def load_plane(queues, plane, scales):
            rows = scales[0].bitcast(I32)
            for q, queue in enumerate(queues):
                four = rows[4 * q : 4 * q + 4, :].unsqueeze(0).to_broadcast([8, 4, T // 4])
                queue.dma_start(plane[32 * q : 32 * (q + 1), :].bitcast(I32), four)

        def load_rows(queues, plane, scales):
            rows = scales[0].bitcast(I32)
            for q, queue in enumerate(queues):
                queue.dma_start(plane[32 * q : 32 * q + 4, :].bitcast(I32), rows[4 * q : 4 * q + 4, :])

        list_a = sb.tile([P, J // 16], U16, name="list_a")
        list_b = sb.tile([P, J // 16], U16, name="list_b")
        x_words = tile([P, T], U32, "x_words")
        x_plane = tile([P, T], U8, "x_plane")
        wa_raw = tile([P, R], U32, "wa_raw")
        wb_raw = tile([P, R // 2], U32, "wb_raw")
        wa_plane_raw = tile([P, R], U8, "wa_plane_raw")
        wb_plane_raw = tile([P, R], U8, "wb_plane_raw")
        bias_raw = tile([P, 2], F32, "bias_raw")
        identity = tile([P, P], F32, "identity")
        lag = [tile([P, HALF, PACK], F32, "lag%d" % h) for h in range(2)]

        nc.vector.memset(wb_plane_raw[:].bitcast(I32), 0)
        nc.vector.memset(wa_plane_raw[:].bitcast(I32), 0)
        nc.vector.memset(lag[0][:, 0, :], 0.0)

        nc.sync.dma_start(list_b[:], offs2)
        load_plane([nc.sync, nc.sync, nc.scalar, nc.scalar], x_plane, xt_scales)
        nc.sync.dma_start(list_a[:], offs)
        nc.scalar.dma_start(x_words[:].bitcast(I32), xt_words[0].rearrange("p n t -> p (n t)").bitcast(I32))
        nc.sync.dma_start(wb_raw[:].bitcast(I32), wb_words[0].bitcast(I32))
        load_rows([nc.sync] * 4, wb_plane_raw, wb_scales)
        nc.sync.dma_start(wa_raw[:].bitcast(I32), wa_words[0].rearrange("p n t -> p (n t)").bitcast(I32))
        load_rows([nc.sync] * 3 + [nc.gpsimd], wa_plane_raw, wa_scales)
        nc.sync.dma_start(bias_raw[:], bi[0].rearrange("(p c) -> p c", c=2))
        make_identity(nc, identity[:])

        xb_words = tile([P, J], U32, "xb_words")
        xb_plane = tile([P, J], U8, "xb_plane")
        xa_words = tile([P, J], U32, "xa_words")
        xa_plane = tile([P, J], U8, "xa_plane")
        nc.vector.tensor_copy(xb_plane[:], x_plane[:].indirect(list_b[:]))
        nc.vector.tensor_copy(xa_plane[:], x_plane[:].indirect(list_a[:]))
        for h in range(2):
            nc.vector.tensor_copy(xb_words[:, HALF * h : HALF * (h + 1)], x_words[:].indirect(list_b[:, 8 * h : 8 * (h + 1)]))
        nc.vector.tensor_copy(xa_words[:], x_words[:].indirect(list_a[:]))

        def deal(dst, src):
            nc.scalar.copy(dst.rearrange("p (t g u) -> p t g u", t=PACK, g=16), src.rearrange("p (g t u) -> p t g u", t=PACK, g=16))

        wb_dealt = tile([P, 2 * R], U8, "wb_dealt")
        wb_plane = tile([P, R], U8, "wb_plane")
        wa_plane = tile([P, R], U8, "wa_plane")
        deal(wb_dealt[:].bitcast(U32), wb_raw[:])
        deal(wb_plane[:].bitcast(U32), wb_plane_raw[:].bitcast(U32))
        wa_dealt = tile([P, R], U32, "wa_dealt")
        deal(wa_dealt[:], wa_raw[:])
        deal(wa_plane[:].bitcast(U32), wa_plane_raw[:].bitcast(U32))

        zb = [ps.tile([P, PACK, HALF], F32, name="zb%d" % h) for h in range(2)]
        za = [ps.tile([P, PACK, HALF], F32, name="za%d" % h) for h in range(2)]
        for h in range(2):
            cols = slice(HALF * h, HALF * (h + 1))
            for t in range(PACK):
                nc.tensor.matmul_mx(
                    out=zb[h][:, t, :],
                    lhsT=wb_dealt[:, 2 * P * t : 2 * P * (t + 1)].bitcast(E2M1),
                    lhsT_scale=wb_plane[:, P * t : P * (t + 1)],
                    rhs=xb_words[:, cols].bitcast(E5M2),
                    rhs_scale=xb_plane[:, cols],
                    start=True,
                    stop=True,
                )
        for h in range(2):
            cols = slice(HALF * h, HALF * (h + 1))
            for t in range(PACK):
                nc.tensor.matmul_mx(
                    out=za[h][:, t, :],
                    lhsT=wa_dealt[:, P * t : P * (t + 1)].bitcast(E4M3),
                    lhsT_scale=wa_plane[:, P * t : P * (t + 1)],
                    rhs=xa_words[:, cols].bitcast(E5M2),
                    rhs_scale=xa_plane[:, cols],
                    start=True,
                    stop=True,
                )

        groups = HALF // BUNDLE
        sums = [tile([P, groups, PACK], F32, "sums%d" % h) for h in range(2)]
        means = [tile([P, groups, PACK], F32, "means%d" % h) for h in range(2)]
        hb = tile([P, J, PACK], BF16, "hb")
        for h in range(2):
            nc.vector.tensor_reduce(
                out=sums[h][:], in_=zb[h][:].rearrange("p t (g u) -> p g t u", u=BUNDLE), axis=AXIS_X, op=ALU.add
            )
            nc.gpsimd.tensor_scalar(means[h][:], sums[h][:], 1.0 / BUNDLE, 0.0, ALU.mult, ALU.add)
        for h in range(2):
            nc.vector.tensor_tensor(
                hb[:, HALF * h : HALF * (h + 1), :].rearrange("p (g u) t -> p g u t", u=BUNDLE),
                zb[h][:].rearrange("p t (g u) -> p g u t", u=BUNDLE),
                means[h][:].unsqueeze(2).to_broadcast([P, groups, BUNDLE, PACK]),
                ALU.subtract,
            )

        nc.scalar.copy(lag[0][:, 1:HALF, :], za[0][:, :, 0 : HALF - 1].rearrange("p t j -> p j t"))
        nc.scalar.copy(lag[1][:, 0, :], za[0][:, :, HALF - 1])
        nc.scalar.copy(lag[1][:, 1:HALF, :], za[1][:, :, 0 : HALF - 1].rearrange("p t j -> p j t"))
        bias_scaled = tile([P, 2], F32, "bias_scaled", tag="wa_plane")
        nc.scalar.activation(bias_scaled[:], bias_raw[:], COPY, scale=0.04)
        spread = ps.tile([P, 2, P], F32, name="spread", tag="score1_1")
        for c in range(2):
            nc.tensor.transpose(spread[:, c, :], bias_scaled[:, c : c + 1].to_broadcast([P, P]), identity[:])
        bias = tile([P, J], F32, "bias")
        nc.scalar.copy(bias[:].rearrange("p (n c) -> p n c", c=2), spread[:].rearrange("p c n -> p n c"))

        ha_codes = [tile([P, HALF], U32, "ha_codes%d" % h) for h in range(2)]
        ha_plane = [tile([P, HALF], U8, "ha_plane%d" % h) for h in range(2)]
        hb_plane = tile([P, J], U8, "hb_plane")
        best = [tile([P, J // BUNDLE], F32, "best%d" % h) for h in range(2)]

        def make_ha(h, tag):
            ha = tile([P, HALF, PACK], BF16, "ha%d" % h, tag=tag)
            nc.vector.scalar_tensor_tensor(
                ha[:], lag[h][:], -0.6, za[h][:].rearrange("p t j -> p j t"), ALU.mult, ALU.add
            )
            return ha

        def quantize_ha(h, ha):
            nc.vector.quantize_mx(out=ha_codes[h][:].bitcast(E5M2), scales=ha_plane[h][:], in_=ha[:].rearrange("p j t -> p (j t)"))

        def meet(h, pieces):
            width = J // pieces
            biased = []
            for c in range(pieces):
                cols = slice(width * c, width * (c + 1))
                score = ps.tile([P, width], F32, name="score%d_%d" % (h, c))
                nc.tensor.matmul_mx(
                    out=score[:],
                    lhsT=ha_codes[h][:].bitcast(E5M2),
                    lhsT_scale=ha_plane[h][:],
                    rhs=hb_codes[:, cols].bitcast(E4M3),
                    rhs_scale=hb_plane[:, cols],
                    start=True,
                    stop=True,
                )
                biased.append(tile([P, width], F32, "biased%d_%d" % (h, c), tag="hb" if (h, c) == (0, 1) else None))
                nc.vector.scalar_tensor_tensor(biased[c][:], score[:], 0.04, bias[:, cols], ALU.mult, ALU.add)
            for c in range(pieces):
                sets = slice(width // BUNDLE * c, width // BUNDLE * (c + 1))
                nc.vector.tensor_reduce(
                    out=best[h][:, sets], in_=biased[c][:].rearrange("p (s u) -> p s u", u=BUNDLE), axis=AXIS_X, op=ALU.max
                )
            nc.sync.dma_start(out[HALF * h : HALF * (h + 1), :], best[h][:])

        ha0 = make_ha(0, "ha0")
        hb_codes = tile([P, J], U32, "hb_codes", tag="lag0")
        nc.vector.quantize_mx(out=hb_codes[:].bitcast(E4M3), scales=hb_plane[:], in_=hb[:].rearrange("p i t -> p (i t)"))
        quantize_ha(0, ha0)
        quantize_ha(1, make_ha(1, "hb"))
        meet(0, 2)
        meet(1, 2)
